import numpy as np, ml_dtypes
CORES = [35,38,43,46]
N = 4
TK, LAY = 128, 2
def setup_inputs(rng):
    return {"x": rng.standard_normal((N, 128, TK), dtype=np.float32).astype(ml_dtypes.bfloat16), "wu": (rng.standard_normal((N, 128, LAY * 256), dtype=np.float32) / 16).astype(ml_dtypes.bfloat16), "wd": (rng.standard_normal((N, 128, 256), dtype=np.float32) / 16).astype(ml_dtypes.bfloat16)}
def setup_inputs_big(rng):
    d = setup_inputs(rng)
    for k in ("x",): d[k] = (d[k].astype(np.float32) * 1048576.0).astype(d[k].dtype)
    return d
def setup_inputs_small(rng):
    d = setup_inputs(rng)
    for k in ("x",): d[k] = (d[k].astype(np.float32) * (1 / 1048576.0)).astype(d[k].dtype)
    return d
def setup_inputs_apart(rng):
    d = setup_inputs(rng)
    f = (10.0 ** rng.permutation(np.linspace(-1.5, 1.5, N))).astype(np.float32).reshape(N, 1, 1)
    for k in ("x",): d[k] = (d[k].astype(np.float32) * f).astype(d[k].dtype)
    return d
def reference(x, wu, wd):
    X, WU, WD = x.astype(np.float64), wu.astype(np.float64), wd.astype(np.float64)
    s = list(X)
    for l in range(LAY):
        for q in range(0, N, 2 << l):
            p = q + (1 << l)
            s[q] = np.maximum(WU[q][:, 256 * l:256 * l + 128].T @ s[q] + WU[q][:, 256 * l + 128:256 * l + 256].T @ s[p], 0.0)
    for l in range(LAY - 1, -1, -1):
        for q in range(0, N, 2 << l):
            p = q + (1 << l)
            s[p] = np.maximum(WD[p][:, 0:128].T @ s[p] + WD[p][:, 128:256].T @ s[q], 0.0)
    return {"y": np.stack(s).astype(ml_dtypes.bfloat16)}

@@ -1,0 +1,183 @@
+from concourse.bass import DstId, RemoteDMATransfer
+from concourse.mybir import AluOpType
+
+TK = 128
+
+SCRATCH = {
+    "own": ("sbuf", [128, 6 * TK], "bfloat16"),
+    "sib": ("sbuf", [128, 5 * TK], "bfloat16"),
+    "cross": ("sbuf", [128, 3 * TK], "bfloat16"),
+    "wdb": ("sbuf", [128, 2 * TK], "bfloat16"),
+    "y0b": ("sbuf", [128, TK], "bfloat16"),
+    "y2b": ("sbuf", [128, TK], "bfloat16"),
+    "yo": ("sbuf", [128, TK], "bfloat16"),
+    "zero": ("sbuf", [128, TK], "float32"),
+    "ps": ("psum", [128, 512], "float32"),
+    "p0": ("psum", [128, 512], "float32"),
+    "p2": ("psum", [128, 512], "float32"),
+    "pf": ("psum", [128, 512], "float32"),
+}
+SEMAPHORES = ["ld_a", "ld_b", "a_sib", "a_sib2", "a_w", "a_x", "sent", "z",
+              "m_s", "v_s", "m_0", "v_0", "m_2", "v_2", "m_f", "done", "st"]
+
+
+def _count(mask):
+    return bin(mask).count("1")
+
+
+def _every_second(mask):
+    engines = [e for e in range(mask.bit_length()) if (mask >> e) & 1]
+    out = 0
+    for e in engines[::2]:
+        out |= 1 << e
+    return out
+
+
+def _col(t, k, n=1):
+    return t[:, k * TK:(k + n) * TK]
+
+
+def rank_program(g, core, T, topo):
+    r = T.rank_of(core)
+    if r is None:
+        return
+    S = T.sem
+    cores = T.cores
+    even = r % 2 == 0
+    low = r < 2
+    sibling = cores[r ^ 1]
+    others = [cores[i] for i in range(4) if (i < 2) != low]
+    partner = [c for c in others if topo.die(c) == topo.die(core)][0]
+    assert topo.chip(sibling) == topo.chip(core) and topo.mates(topo.chip(core), topo.chip(partner))
+    assert topo.may_write(core, partner) and topo.may_write(core, sibling)
+    far = topo.mask(core, partner)
+    near = topo.mask(core, sibling)
+    near_only = near & ~far
+    sent = [0]
+
+    def send(dst, out_ap, in_ap, sem, mask):
+        rid, pid, _ = topo.addr(dst)
+        g.remote_dma(out_ap, in_ap, remote_sem=sem, local_sem=S.sent, pid=pid, routing_id=rid, dma_engine_mask=mask)
+        sent[0] += _count(mask)
+
+    def relu(out, acc, sem):
+        g.vector.tensor_tensor(out, acc[:, 0:TK], T.zero[:], AluOpType.max).then_inc(sem, 1)
+
+    def mm(acc, w, s, start, stop):
+        return g.tensor.matmul(acc[:, 0:TK], w, s, start=start, stop=stop)
+
+    own, sib, cross = T.own, T.sib, T.cross
+    s_loc, s_far = _col(own, 3), _col(cross, 0)
+
+    g.sync.dma_start(_col(own, 0), T.x[:, :]).then_inc(S.ld_a, 16)
+    if even:
+        g.scalar.dma_start(_col(own, 1, 2), T.wu[:, 0:2 * TK]).then_inc(S.ld_a, 16)
+        later = T.wu[:, 2 * TK:4 * TK] if r == 0 else T.wd[:, :]
+        g.sync.dma_start(_col(own, 4, 2), later).then_inc(S.ld_b, 16)
+    else:
+        g.scalar.dma_start(T.wdb[:, :], T.wd[:, :]).then_inc(S.ld_b, 16)
+    n_a = 32 if even else 16
+    g.vector.memset(T.zero[:], 0.0).then_inc(S.z, 1)
+
+    n_sib_even = _count(_every_second(near))
+    n_far = _count(far)
+    g.wait_ge(S.ld_a, n_a)
+    if even:
+        send(sibling, _col(sib, 0, 3), _col(own, 0, 3), S.a_sib, _every_second(near))
+        g.wait_ge(S.ld_b, 16)
+        if r == 0:
+            r3 = [c for c in others if c != partner][0]
+            assert topo.may_write(core, r3)
+            rid1, pid1, _ = topo.addr(sibling)
+            rid3, pid3, _ = topo.addr(r3)
+            g.remote_dma_fused([
+                RemoteDMATransfer(dst_ids=[DstId(rid=rid3, pnc=pid3)], dma_engine_mask=topo.mask(core, r3),
+                                  remote_sem=S.a_w, src=_col(own, 4, 2), dst=_col(cross, 1, 2)),
+                RemoteDMATransfer(dst_ids=[DstId(rid=rid1, pnc=pid1)], dma_engine_mask=near & ~topo.mask(core, r3),
+                                  remote_sem=S.a_sib2, src=_col(own, 4, 2), dst=_col(sib, 3, 2)),
+            ], local_sem=S.sent)
+            sent[0] += _count(topo.mask(core, r3)) + _count(near & ~topo.mask(core, r3))
+        else:
+            send(sibling, _col(sib, 3, 2), _col(own, 4, 2), S.a_sib2, far & near)
+        g.wait_ge(S.v_s, 1)
+        if r == 0:
+            send(partner, _col(cross, 0, 3), _col(own, 3, 3), S.a_x, far)
+        else:
+            send(partner, s_far, s_loc, S.a_x, far)
+    else:
+        send(sibling, _col(sib, 0), _col(own, 0), S.a_sib, far & near)
+        g.wait_ge(S.v_s, 1)
+        send(partner, s_far, s_loc, S.a_x, far)
+    g.wait_ge(S.sent, sent[0])
+
+    te = g.tensor
+    te.wait_ge(S.ld_a, n_a)
+    if even:
+        mm(T.ps, _col(own, 1), _col(own, 0), True, False)
+        te.wait_ge(S.a_sib, n_far)
+        mm(T.ps, _col(own, 2), _col(sib, 0), False, True).then_inc(S.m_s, 1)
+    else:
+        te.wait_ge(S.ld_b, 16)
+        mm(T.pf, _col(T.wdb, 0), _col(own, 0), True, False)
+        te.wait_ge(S.a_sib, n_sib_even)
+        mm(T.ps, _col(sib, 1), _col(sib, 0), True, False)
+        mm(T.ps, _col(sib, 2), _col(own, 0), False, True).then_inc(S.m_s, 1)
+    te.wait_ge(S.v_s, 1)
+    if low:
+        if even:
+            te.wait_ge(S.ld_b, 16)
+            u1, v1 = _col(own, 4), _col(own, 5)
+        else:
+            te.wait_ge(S.a_sib2, _count(near_only))
+            u1, v1 = _col(sib, 3), _col(sib, 4)
+        mm(T.p0, u1, s_loc, True, False)
+        te.wait_ge(S.a_x, n_far)
+        mm(T.p0, v1, s_far, False, True).then_inc(S.m_0, 1)
+    else:
+        u1, v1 = _col(cross, 1), _col(cross, 2)
+        if even:
+            te.wait_ge(S.ld_b, 16)
+            d2, e2 = _col(own, 4), _col(own, 5)
+            mm(T.p2, d2, s_loc, True, False)
+            te.wait_ge(S.a_x, n_far)
+            mm(T.p0, v1, s_loc, True, False)
+        else:
+            te.wait_ge(S.a_w, n_far)
+            mm(T.p0, v1, s_loc, True, False)
+            te.wait_ge(S.a_sib2, n_far)
+            d2, e2 = _col(sib, 3), _col(sib, 4)
+            mm(T.p2, d2, s_loc, True, False)
+            te.wait_ge(S.a_x, n_far)
+        mm(T.p0, u1, s_far, False, True).then_inc(S.m_0, 1)
+        te.wait_ge(S.v_0, 1)
+        mm(T.p2, e2, T.y0b[:], False, True).then_inc(S.m_2, 1)
+    if not even:
+        if low:
+            te.wait_ge(S.v_0, 1)
+            mm(T.pf, _col(T.wdb, 1), T.y0b[:], False, True).then_inc(S.m_f, 1)
+        else:
+            te.wait_ge(S.v_2, 1)
+            mm(T.pf, _col(T.wdb, 1), T.y2b[:], False, True).then_inc(S.m_f, 1)
+
+    ve = g.vector
+    ve.wait_ge(S.z, 1)
+    ve.wait_ge(S.m_s, 1)
+    relu(s_loc, T.ps, S.v_s)
+    ve.wait_ge(S.m_0, 1)
+    if r == 0:
+        relu(T.yo[:], T.p0, S.done)
+    else:
+        relu(T.y0b[:], T.p0, S.v_0)
+        if not low:
+            ve.wait_ge(S.m_2, 1)
+            if even:
+                relu(T.yo[:], T.p2, S.done)
+            else:
+                relu(T.y2b[:], T.p2, S.v_2)
+        if not even:
+            ve.wait_ge(S.m_f, 1)
+            relu(T.yo[:], T.pf, S.done)
+
+    g.sync.wait_ge(S.done, 1)
+    g.sync.dma_start(T.y[:, :], T.yo[:]).then_inc(S.st, 16)
+    g.sync.wait_ge(S.st, 16)

@@ -4,33 +4,29 @@ from concourse.mybir import AluOpType
 TK = 128
 
 SCRATCH = {
-    "own": ("sbuf", [128, 6 * TK], "bfloat16"),
-    "sib": ("sbuf", [128, 5 * TK], "bfloat16"),
-    "cross": ("sbuf", [128, 3 * TK], "bfloat16"),
-    "wdb": ("sbuf", [128, 2 * TK], "bfloat16"),
+    "own": ("sbuf", [128, 5 * TK], "bfloat16"),
+    "xd": ("dram", [128, TK], "bfloat16"),
+    "rawA": ("sbuf", [128, 5 * TK], "bfloat16"),
+    "rawB": ("sbuf", [128, 5 * TK], "bfloat16"),
+    "xs": ("sbuf", [128, TK], "bfloat16"),
+    "ta": ("sbuf", [128, TK], "bfloat16"),
+    "tb": ("sbuf", [128, TK], "bfloat16"),
     "y0b": ("sbuf", [128, TK], "bfloat16"),
     "y2b": ("sbuf", [128, TK], "bfloat16"),
     "yo": ("sbuf", [128, TK], "bfloat16"),
     "zero": ("sbuf", [128, TK], "float32"),
-    "ps": ("psum", [128, 512], "float32"),
+    "pa": ("psum", [128, 512], "float32"),
+    "pb": ("psum", [128, 512], "float32"),
     "p0": ("psum", [128, 512], "float32"),
     "p2": ("psum", [128, 512], "float32"),
     "pf": ("psum", [128, 512], "float32"),
 }
-SEMAPHORES = ["ld_a", "ld_b", "a_sib", "a_sib2", "a_w", "a_x", "sent", "z",
-              "m_s", "v_s", "m_0", "v_0", "m_2", "v_2", "m_f", "done", "st"]
+SEMAPHORES = ["ld_x", "ld_a", "a_xs", "a_w", "a_rb", "a_ta", "a_tb", "sent", "z",
+              "m_a", "v_a", "m_b", "v_b", "m_0", "v_0", "m_2", "v_2", "m_f", "done", "st"]
 
 
 def _count(mask):
     return bin(mask).count("1")
-
-
-def _every_second(mask):
-    engines = [e for e in range(mask.bit_length()) if (mask >> e) & 1]
-    out = 0
-    for e in engines[::2]:
-        out |= 1 << e
-    return out
 
 
 def _col(t, k, n=1):
@@ -43,16 +39,15 @@ def rank_program(g, core, T, topo):
         return
     S = T.sem
     cores = T.cores
-    even = r % 2 == 0
-    low = r < 2
     sibling = cores[r ^ 1]
-    others = [cores[i] for i in range(4) if (i < 2) != low]
-    partner = [c for c in others if topo.die(c) == topo.die(core)][0]
-    assert topo.chip(sibling) == topo.chip(core) and topo.mates(topo.chip(core), topo.chip(partner))
-    assert topo.may_write(core, partner) and topo.may_write(core, sibling)
-    far = topo.mask(core, partner)
+    others = [cores[i] for i in range(4) if (i < 2) != (r < 2)]
+    assert topo.chip(sibling) == topo.chip(core)
+    for c in others:
+        assert topo.mates(topo.chip(core), topo.chip(c)) and topo.may_write(core, c)
+    far = topo.mask(core, others[0])
     near = topo.mask(core, sibling)
     near_only = near & ~far
+    n_far, n_near, n_only = _count(far), _count(near), _count(near_only)
     sent = [0]
 
     def send(dst, out_ap, in_ap, sem, mask):
@@ -60,124 +55,133 @@ def rank_program(g, core, T, topo):
         g.remote_dma(out_ap, in_ap, remote_sem=sem, local_sem=S.sent, pid=pid, routing_id=rid, dma_engine_mask=mask)
         sent[0] += _count(mask)
 
+    def fused(parts):
+        trs = []
+        for dst, out_ap, in_ap, sem, mask in parts:
+            rid, pid, _ = topo.addr(dst)
+            trs.append(RemoteDMATransfer(dst_ids=[DstId(rid=rid, pnc=pid)], dma_engine_mask=mask,
+                                         remote_sem=sem, src=in_ap, dst=out_ap))
+            sent[0] += _count(mask)
+        g.remote_dma_fused(trs, local_sem=S.sent)
+
     def relu(out, acc, sem):
         g.vector.tensor_tensor(out, acc[:, 0:TK], T.zero[:], AluOpType.max).then_inc(sem, 1)
 
     def mm(acc, w, s, start, stop):
         return g.tensor.matmul(acc[:, 0:TK], w, s, start=start, stop=stop)
 
-    own, sib, cross = T.own, T.sib, T.cross
-    s_loc, s_far = _col(own, 3), _col(cross, 0)
-
-    g.sync.dma_start(_col(own, 0), T.x[:, :]).then_inc(S.ld_a, 16)
-    if even:
-        g.scalar.dma_start(_col(own, 1, 2), T.wu[:, 0:2 * TK]).then_inc(S.ld_a, 16)
-        later = T.wu[:, 2 * TK:4 * TK] if r == 0 else T.wd[:, :]
-        g.sync.dma_start(_col(own, 4, 2), later).then_inc(S.ld_b, 16)
-    else:
-        g.scalar.dma_start(T.wdb[:, :], T.wd[:, :]).then_inc(S.ld_b, 16)
-    n_a = 32 if even else 16
-    g.vector.memset(T.zero[:], 0.0).then_inc(S.z, 1)
-
-    n_sib_even = _count(_every_second(near))
-    n_far = _count(far)
-    g.wait_ge(S.ld_a, n_a)
-    if even:
-        send(sibling, _col(sib, 0, 3), _col(own, 0, 3), S.a_sib, _every_second(near))
-        g.wait_ge(S.ld_b, 16)
-        if r == 0:
-            r3 = [c for c in others if c != partner][0]
-            assert topo.may_write(core, r3)
-            rid1, pid1, _ = topo.addr(sibling)
-            rid3, pid3, _ = topo.addr(r3)
-            g.remote_dma_fused([
-                RemoteDMATransfer(dst_ids=[DstId(rid=rid3, pnc=pid3)], dma_engine_mask=topo.mask(core, r3),
-                                  remote_sem=S.a_w, src=_col(own, 4, 2), dst=_col(cross, 1, 2)),
-                RemoteDMATransfer(dst_ids=[DstId(rid=rid1, pnc=pid1)], dma_engine_mask=near & ~topo.mask(core, r3),
-                                  remote_sem=S.a_sib2, src=_col(own, 4, 2), dst=_col(sib, 3, 2)),
-            ], local_sem=S.sent)
-            sent[0] += _count(topo.mask(core, r3)) + _count(near & ~topo.mask(core, r3))
-        else:
-            send(sibling, _col(sib, 3, 2), _col(own, 4, 2), S.a_sib2, far & near)
-        g.wait_ge(S.v_s, 1)
-        if r == 0:
-            send(partner, _col(cross, 0, 3), _col(own, 3, 3), S.a_x, far)
-        else:
-            send(partner, s_far, s_loc, S.a_x, far)
-    else:
-        send(sibling, _col(sib, 0), _col(own, 0), S.a_sib, far & near)
-        g.wait_ge(S.v_s, 1)
-        send(partner, s_far, s_loc, S.a_x, far)
-    g.wait_ge(S.sent, sent[0])
-
-    te = g.tensor
-    te.wait_ge(S.ld_a, n_a)
-    if even:
-        mm(T.ps, _col(own, 1), _col(own, 0), True, False)
-        te.wait_ge(S.a_sib, n_far)
-        mm(T.ps, _col(own, 2), _col(sib, 0), False, True).then_inc(S.m_s, 1)
-    else:
-        te.wait_ge(S.ld_b, 16)
-        mm(T.pf, _col(T.wdb, 0), _col(own, 0), True, False)
-        te.wait_ge(S.a_sib, n_sib_even)
-        mm(T.ps, _col(sib, 1), _col(sib, 0), True, False)
-        mm(T.ps, _col(sib, 2), _col(own, 0), False, True).then_inc(S.m_s, 1)
-    te.wait_ge(S.v_s, 1)
-    if low:
-        if even:
-            te.wait_ge(S.ld_b, 16)
-            u1, v1 = _col(own, 4), _col(own, 5)
-        else:
-            te.wait_ge(S.a_sib2, _count(near_only))
-            u1, v1 = _col(sib, 3), _col(sib, 4)
-        mm(T.p0, u1, s_loc, True, False)
-        te.wait_ge(S.a_x, n_far)
-        mm(T.p0, v1, s_far, False, True).then_inc(S.m_0, 1)
-    else:
-        u1, v1 = _col(cross, 1), _col(cross, 2)
-        if even:
-            te.wait_ge(S.ld_b, 16)
-            d2, e2 = _col(own, 4), _col(own, 5)
-            mm(T.p2, d2, s_loc, True, False)
-            te.wait_ge(S.a_x, n_far)
-            mm(T.p0, v1, s_loc, True, False)
-        else:
-            te.wait_ge(S.a_w, n_far)
-            mm(T.p0, v1, s_loc, True, False)
-            te.wait_ge(S.a_sib2, n_far)
-            d2, e2 = _col(sib, 3), _col(sib, 4)
-            mm(T.p2, d2, s_loc, True, False)
-            te.wait_ge(S.a_x, n_far)
-        mm(T.p0, u1, s_far, False, True).then_inc(S.m_0, 1)
-        te.wait_ge(S.v_0, 1)
-        mm(T.p2, e2, T.y0b[:], False, True).then_inc(S.m_2, 1)
-    if not even:
-        if low:
-            te.wait_ge(S.v_0, 1)
-            mm(T.pf, _col(T.wdb, 1), T.y0b[:], False, True).then_inc(S.m_f, 1)
-        else:
-            te.wait_ge(S.v_2, 1)
-            mm(T.pf, _col(T.wdb, 1), T.y2b[:], False, True).then_inc(S.m_f, 1)
-
-    ve = g.vector
+    own, rawA, rawB = T.own, T.rawA, T.rawB
+    ta, tb, xs = T.ta[:], T.tb[:], T.xs[:]
+    te, ve = g.tensor, g.vector
+    ve.memset(T.zero[:], 0.0).then_inc(S.z, 1)
     ve.wait_ge(S.z, 1)
-    ve.wait_ge(S.m_s, 1)
-    relu(s_loc, T.ps, S.v_s)
-    ve.wait_ge(S.m_0, 1)
-    if r == 0:
-        relu(T.yo[:], T.p0, S.done)
-    else:
-        relu(T.y0b[:], T.p0, S.v_0)
-        if not low:
-            ve.wait_ge(S.m_2, 1)
-            if even:
-                relu(T.yo[:], T.p2, S.done)
-            else:
-                relu(T.y2b[:], T.p2, S.v_2)
-        if not even:
-            ve.wait_ge(S.m_f, 1)
-            relu(T.yo[:], T.pf, S.done)
 
+    if r == 0:
+        g.sync.dma_start(_col(own, 0), T.x[:, :]).then_inc(S.ld_a, 16)
+        g.scalar.dma_start(_col(own, 1, 4), T.wu[:, :]).then_inc(S.ld_a, 16)
+        g.wait_ge(S.ld_a, 32)
+        send(cores[3], _col(rawA, 0, 5), _col(own, 0, 5), S.a_w, far)
+        fused([(cores[2], _col(rawA, 3, 2), _col(own, 3, 2), S.a_w, far),
+               (cores[1], _col(rawA, 3, 2), _col(own, 3, 2), S.a_w, near_only)])
+        g.wait_ge(S.v_a, 1)
+        fused([(cores[2], ta, ta, S.a_ta, far), (cores[1], ta, ta, S.a_ta, near_only)])
+
+        te.wait_ge(S.ld_a, 32)
+        mm(T.pa, _col(own, 1), _col(own, 0), True, False)
+        te.wait_ge(S.a_xs, n_far)
+        mm(T.pa, _col(own, 2), xs, False, True).then_inc(S.m_a, 1)
+        te.wait_ge(S.v_a, 1)
+        mm(T.p0, _col(own, 3), ta, True, False)
+        te.wait_ge(S.a_tb, n_far)
+        mm(T.p0, _col(own, 4), tb, False, True).then_inc(S.m_0, 1)
+
+        ve.wait_ge(S.m_a, 1)
+        relu(ta, T.pa, S.v_a)
+        ve.wait_ge(S.m_0, 1)
+        relu(T.yo[:], T.p0, S.done)
+
+    elif r == 2:
+        g.sync.dma_start(_col(own, 0), T.x[:, :]).then_inc(S.ld_a, 16)
+        g.scalar.dma_start(_col(own, 1, 2), T.wu[:, 0:2 * TK]).then_inc(S.ld_a, 16)
+        g.sync.dma_start(_col(own, 3, 2), T.wd[:, :]).then_inc(S.ld_a, 16)
+        g.wait_ge(S.ld_a, 48)
+        send(cores[3], _col(rawB, 0, 5), _col(own, 0, 5), S.a_rb, near)
+        g.wait_ge(S.v_b, 1)
+        send(cores[1], tb, tb, S.a_tb, far)
+        send(cores[0], tb, tb, S.a_tb, far)
+
+        te.wait_ge(S.ld_a, 48)
+        mm(T.pb, _col(own, 1), _col(own, 0), True, False)
+        te.wait_ge(S.a_xs, n_far)
+        mm(T.pb, _col(own, 2), xs, False, True).then_inc(S.m_b, 1)
+        te.wait_ge(S.v_b, 1)
+        mm(T.p2, _col(own, 3), tb, True, False)
+        te.wait_ge(S.a_w, n_far)
+        mm(T.p0, _col(rawA, 4), tb, True, False)
+        te.wait_ge(S.a_ta, n_far)
+        mm(T.p0, _col(rawA, 3), ta, False, True).then_inc(S.m_0, 1)
+        te.wait_ge(S.v_0, 1)
+        mm(T.p2, _col(own, 4), T.y0b[:], False, True).then_inc(S.m_2, 1)
+
+        ve.wait_ge(S.m_b, 1)
+        relu(tb, T.pb, S.v_b)
+        ve.wait_ge(S.m_0, 1)
+        relu(T.y0b[:], T.p0, S.v_0)
+        ve.wait_ge(S.m_2, 1)
+        relu(T.yo[:], T.p2, S.done)
+
+    else:
+        g.sync.dma_start(T.xd[:, :], T.x[:, :]).then_inc(S.ld_x, 16)
+        g.scalar.dma_start(_col(own, 0), T.x[:, :]).then_inc(S.ld_a, 16)
+        g.sync.dma_start(_col(own, 1, 2), T.wd[:, :]).then_inc(S.ld_a, 16)
+        g.wait_ge(S.ld_x, 16)
+        send(sibling, xs, T.xd[:, :], S.a_xs, far & near)
+        if r == 1:
+            send(cores[3], xs, T.xd[:, :], S.a_xs, far)
+
+        te.wait_ge(S.ld_a, 32)
+        mm(T.pf, _col(own, 1), _col(own, 0), True, False)
+        if r == 1:
+            te.wait_ge(S.a_w, n_only)
+            te.wait_ge(S.a_ta, n_only)
+            mm(T.p0, _col(rawA, 3), ta, True, False)
+            te.wait_ge(S.a_tb, n_far)
+            mm(T.p0, _col(rawA, 4), tb, False, True).then_inc(S.m_0, 1)
+            te.wait_ge(S.v_0, 1)
+            mm(T.pf, _col(own, 2), T.y0b[:], False, True).then_inc(S.m_f, 1)
+
+            ve.wait_ge(S.m_0, 1)
+            relu(T.y0b[:], T.p0, S.v_0)
+        else:
+            te.wait_ge(S.a_rb, n_near)
+            mm(T.pb, _col(rawB, 1), _col(rawB, 0), True, False)
+            mm(T.pb, _col(rawB, 2), _col(own, 0), False, True).then_inc(S.m_b, 1)
+            te.wait_ge(S.a_w, n_far)
+            te.wait_ge(S.a_xs, n_far)
+            mm(T.pa, _col(rawA, 1), _col(rawA, 0), True, False)
+            mm(T.pa, _col(rawA, 2), xs, False, True).then_inc(S.m_a, 1)
+            te.wait_ge(S.v_b, 1)
+            mm(T.p2, _col(rawB, 3), tb, True, False)
+            mm(T.p0, _col(rawA, 4), tb, True, False)
+            te.wait_ge(S.v_a, 1)
+            mm(T.p0, _col(rawA, 3), ta, False, True).then_inc(S.m_0, 1)
+            te.wait_ge(S.v_0, 1)
+            mm(T.p2, _col(rawB, 4), T.y0b[:], False, True).then_inc(S.m_2, 1)
+            te.wait_ge(S.v_2, 1)
+            mm(T.pf, _col(own, 2), T.y2b[:], False, True).then_inc(S.m_f, 1)
+
+            ve.wait_ge(S.m_b, 1)
+            relu(tb, T.pb, S.v_b)
+            ve.wait_ge(S.m_a, 1)
+            relu(ta, T.pa, S.v_a)
+            ve.wait_ge(S.m_0, 1)
+            relu(T.y0b[:], T.p0, S.v_0)
+            ve.wait_ge(S.m_2, 1)
+            relu(T.y2b[:], T.p2, S.v_2)
+        ve.wait_ge(S.m_f, 1)
+        relu(T.yo[:], T.pf, S.done)
+
+    g.wait_ge(S.sent, sent[0])
     g.sync.wait_ge(S.done, 1)
     g.sync.dma_start(T.y[:, :], T.yo[:]).then_inc(S.st, 16)
     g.sync.wait_ge(S.st, 16)

from concourse.bass import DstId, RemoteDMATransfer
from concourse.mybir import AluOpType

TK = 128

SCRATCH = {
    "own": ("sbuf", [128, 5 * TK], "bfloat16"),
    "xd": ("dram", [128, TK], "bfloat16"),
    "rawA": ("sbuf", [128, 5 * TK], "bfloat16"),
    "rawB": ("sbuf", [128, 5 * TK], "bfloat16"),
    "xs": ("sbuf", [128, TK], "bfloat16"),
    "ta": ("sbuf", [128, TK], "bfloat16"),
    "tb": ("sbuf", [128, TK], "bfloat16"),
    "y0b": ("sbuf", [128, TK], "bfloat16"),
    "y2b": ("sbuf", [128, TK], "bfloat16"),
    "yo": ("sbuf", [128, TK], "bfloat16"),
    "zero": ("sbuf", [128, TK], "float32"),
    "pa": ("psum", [128, 512], "float32"),
    "pb": ("psum", [128, 512], "float32"),
    "p0": ("psum", [128, 512], "float32"),
    "p2": ("psum", [128, 512], "float32"),
    "pf": ("psum", [128, 512], "float32"),
}
SEMAPHORES = ["ld_x", "ld_a", "a_xs", "a_w", "a_rb", "a_ta", "a_tb", "sent", "z",
              "m_a", "v_a", "m_b", "v_b", "m_0", "v_0", "m_2", "v_2", "m_f", "done", "st"]


def _count(mask):
    return bin(mask).count("1")


def _col(t, k, n=1):
    return t[:, k * TK:(k + n) * TK]


def rank_program(g, core, T, topo):
    r = T.rank_of(core)
    if r is None:
        return
    S = T.sem
    cores = T.cores
    sibling = cores[r ^ 1]
    others = [cores[i] for i in range(4) if (i < 2) != (r < 2)]
    assert topo.chip(sibling) == topo.chip(core)
    for c in others:
        assert topo.mates(topo.chip(core), topo.chip(c)) and topo.may_write(core, c)
    far = topo.mask(core, others[0])
    near = topo.mask(core, sibling)
    near_only = near & ~far
    n_far, n_near, n_only = _count(far), _count(near), _count(near_only)
    sent = [0]

    def send(dst, out_ap, in_ap, sem, mask):
        rid, pid, _ = topo.addr(dst)
        g.remote_dma(out_ap, in_ap, remote_sem=sem, local_sem=S.sent, pid=pid, routing_id=rid, dma_engine_mask=mask)
        sent[0] += _count(mask)

    def fused(parts):
        trs = []
        for dst, out_ap, in_ap, sem, mask in parts:
            rid, pid, _ = topo.addr(dst)
            trs.append(RemoteDMATransfer(dst_ids=[DstId(rid=rid, pnc=pid)], dma_engine_mask=mask,
                                         remote_sem=sem, src=in_ap, dst=out_ap))
            sent[0] += _count(mask)
        g.remote_dma_fused(trs, local_sem=S.sent)

    def relu(out, acc, sem):
        g.vector.tensor_tensor(out, acc[:, 0:TK], T.zero[:], AluOpType.max).then_inc(sem, 1)

    def mm(acc, w, s, start, stop):
        return g.tensor.matmul(acc[:, 0:TK], w, s, start=start, stop=stop)

    own, rawA, rawB = T.own, T.rawA, T.rawB
    ta, tb, xs = T.ta[:], T.tb[:], T.xs[:]
    te, ve = g.tensor, g.vector
    ve.memset(T.zero[:], 0.0).then_inc(S.z, 1)
    ve.wait_ge(S.z, 1)

    if r == 0:
        g.sync.dma_start(_col(own, 0), T.x[:, :]).then_inc(S.ld_a, 16)
        g.scalar.dma_start(_col(own, 1, 4), T.wu[:, :]).then_inc(S.ld_a, 16)
        g.wait_ge(S.ld_a, 32)
        send(cores[3], _col(rawA, 0, 5), _col(own, 0, 5), S.a_w, far)
        fused([(cores[2], _col(rawA, 3, 2), _col(own, 3, 2), S.a_w, far),
               (cores[1], _col(rawA, 3, 2), _col(own, 3, 2), S.a_w, near_only)])
        g.wait_ge(S.v_a, 1)
        fused([(cores[2], ta, ta, S.a_ta, far), (cores[1], ta, ta, S.a_ta, near_only)])

        te.wait_ge(S.ld_a, 32)
        mm(T.pa, _col(own, 1), _col(own, 0), True, False)
        te.wait_ge(S.a_xs, n_far)
        mm(T.pa, _col(own, 2), xs, False, True).then_inc(S.m_a, 1)
        te.wait_ge(S.v_a, 1)
        mm(T.p0, _col(own, 3), ta, True, False)
        te.wait_ge(S.a_tb, n_far)
        mm(T.p0, _col(own, 4), tb, False, True).then_inc(S.m_0, 1)

        ve.wait_ge(S.m_a, 1)
        relu(ta, T.pa, S.v_a)
        ve.wait_ge(S.m_0, 1)
        relu(T.yo[:], T.p0, S.done)

    elif r == 2:
        g.sync.dma_start(_col(own, 0), T.x[:, :]).then_inc(S.ld_a, 16)
        g.scalar.dma_start(_col(own, 1, 2), T.wu[:, 0:2 * TK]).then_inc(S.ld_a, 16)
        g.sync.dma_start(_col(own, 3, 2), T.wd[:, :]).then_inc(S.ld_a, 16)
        g.wait_ge(S.ld_a, 48)
        send(cores[3], _col(rawB, 0, 5), _col(own, 0, 5), S.a_rb, near)
        g.wait_ge(S.v_b, 1)
        send(cores[1], tb, tb, S.a_tb, far)
        send(cores[0], tb, tb, S.a_tb, far)

        te.wait_ge(S.ld_a, 48)
        mm(T.pb, _col(own, 1), _col(own, 0), True, False)
        te.wait_ge(S.a_xs, n_far)
        mm(T.pb, _col(own, 2), xs, False, True).then_inc(S.m_b, 1)
        te.wait_ge(S.v_b, 1)
        mm(T.p2, _col(own, 3), tb, True, False)
        te.wait_ge(S.a_w, n_far)
        mm(T.p0, _col(rawA, 4), tb, True, False)
        te.wait_ge(S.a_ta, n_far)
        mm(T.p0, _col(rawA, 3), ta, False, True).then_inc(S.m_0, 1)
        te.wait_ge(S.v_0, 1)
        mm(T.p2, _col(own, 4), T.y0b[:], False, True).then_inc(S.m_2, 1)

        ve.wait_ge(S.m_b, 1)
        relu(tb, T.pb, S.v_b)
        ve.wait_ge(S.m_0, 1)
        relu(T.y0b[:], T.p0, S.v_0)
        ve.wait_ge(S.m_2, 1)
        relu(T.yo[:], T.p2, S.done)

    else:
        g.sync.dma_start(T.xd[:, :], T.x[:, :]).then_inc(S.ld_x, 16)
        g.scalar.dma_start(_col(own, 0), T.x[:, :]).then_inc(S.ld_a, 16)
        g.sync.dma_start(_col(own, 1, 2), T.wd[:, :]).then_inc(S.ld_a, 16)
        g.wait_ge(S.ld_x, 16)
        send(sibling, xs, T.xd[:, :], S.a_xs, far & near)
        if r == 1:
            send(cores[3], xs, T.xd[:, :], S.a_xs, far)

        te.wait_ge(S.ld_a, 32)
        mm(T.pf, _col(own, 1), _col(own, 0), True, False)
        if r == 1:
            te.wait_ge(S.a_w, n_only)
            te.wait_ge(S.a_ta, n_only)
            mm(T.p0, _col(rawA, 3), ta, True, False)
            te.wait_ge(S.a_tb, n_far)
            mm(T.p0, _col(rawA, 4), tb, False, True).then_inc(S.m_0, 1)
            te.wait_ge(S.v_0, 1)
            mm(T.pf, _col(own, 2), T.y0b[:], False, True).then_inc(S.m_f, 1)

            ve.wait_ge(S.m_0, 1)
            relu(T.y0b[:], T.p0, S.v_0)
        else:
            te.wait_ge(S.a_rb, n_near)
            mm(T.pb, _col(rawB, 1), _col(rawB, 0), True, False)
            mm(T.pb, _col(rawB, 2), _col(own, 0), False, True).then_inc(S.m_b, 1)
            te.wait_ge(S.a_w, n_far)
            te.wait_ge(S.a_xs, n_far)
            mm(T.pa, _col(rawA, 1), _col(rawA, 0), True, False)
            mm(T.pa, _col(rawA, 2), xs, False, True).then_inc(S.m_a, 1)
            te.wait_ge(S.v_b, 1)
            mm(T.p2, _col(rawB, 3), tb, True, False)
            mm(T.p0, _col(rawA, 4), tb, True, False)
            te.wait_ge(S.v_a, 1)
            mm(T.p0, _col(rawA, 3), ta, False, True).then_inc(S.m_0, 1)
            te.wait_ge(S.v_0, 1)
            mm(T.p2, _col(rawB, 4), T.y0b[:], False, True).then_inc(S.m_2, 1)
            te.wait_ge(S.v_2, 1)
            mm(T.pf, _col(own, 2), T.y2b[:], False, True).then_inc(S.m_f, 1)

            ve.wait_ge(S.m_b, 1)
            relu(tb, T.pb, S.v_b)
            ve.wait_ge(S.m_a, 1)
            relu(ta, T.pa, S.v_a)
            ve.wait_ge(S.m_0, 1)
            relu(T.y0b[:], T.p0, S.v_0)
            ve.wait_ge(S.m_2, 1)
            relu(T.y2b[:], T.p2, S.v_2)
        ve.wait_ge(S.m_f, 1)
        relu(T.yo[:], T.pf, S.done)

    g.wait_ge(S.sent, sent[0])
    g.sync.wait_ge(S.done, 1)
    g.sync.dma_start(T.y[:, :], T.yo[:]).then_inc(S.st, 16)
    g.sync.wait_ge(S.st, 16)
